import numpy as np
import ml_dtypes


def mxq(x, axis, fmt="e4m3"):
    dtype, down = {"e4m3": (ml_dtypes.float8_e4m3fn, 7), "e5m2": (ml_dtypes.float8_e5m2, 14)}[fmt]
    v = np.moveaxis(np.asarray(x, np.float32).astype(ml_dtypes.bfloat16).astype(np.float64), axis, -1)
    blocks = v.reshape(v.shape[:-1] + (-1, 32))
    amax = np.abs(blocks).max(-1, keepdims=True)
    byte = np.maximum(np.where(amax > 0, np.frexp(amax)[1] - 1 + 127, 0) - down, 1)
    scale = np.exp2(byte - 127.0)
    codes = (blocks / scale).astype(np.float32).astype(dtype).astype(np.float64)
    return np.moveaxis((codes * scale).reshape(v.shape), -1, axis)


WIDE = False


def mx_kscale(k):
    if not WIDE:
        return np.ones(k)
    levels = np.array([10, -10, 5, -5, 0])
    if k % 512:
        return np.exp2(np.random.permutation(np.resize(levels, k // 32))).repeat(32)
    a = np.empty((k // 512, 16))
    for p in range(k // 512):
        a[p, :8] = np.random.permutation(np.resize(levels, 8))
        for g in range(8):
            far = levels[np.abs(levels - a[p, g]) >= 10]
            a[p, g + 8] = far[np.random.randint(len(far))]
    return np.exp2(a.ravel()).repeat(32)


def f64(x):
    return np.asarray(x).astype(np.float64)


def striped(idx):
    return np.tile(idx.reshape(-1, 16).T, (8, 1)).astype(np.uint16)


def unstriped(offs):
    return offs[:16].T.reshape(-1).astype(np.int64)


def silu(v):
    return v / (1.0 + np.exp(-np.maximum(v, -700.0)))


K, T, E, C, N = 512, 512, 4, 256, 128


def by_expert(wq, xq):
    return np.concatenate([wq[e].T @ xq[:, e * C:(e + 1) * C] for e in range(E)], axis=1)


def setup_inputs():
    n = np.random.standard_normal
    s = mx_kscale(K)[:, None]
    first = np.random.permutation(np.repeat(np.arange(E), T // E))
    second = (first + 1 + np.random.permutation(np.repeat(np.arange(E - 1), -(-T // (E - 1)))[:T])) % E
    while np.bincount(second, minlength=E).max() != T // E:
        load = np.bincount(second, minlength=E); hi, lo = int(load.argmax()), int(load.argmin())
        t = np.flatnonzero((second == hi) & (first != lo))[0]; second[t] = lo
    slot_token = np.empty(E * C, np.int64); pos = np.empty((2, T), np.int64); fill = np.zeros(E, np.int64)
    place = np.stack([np.random.permutation(C) for _ in range(E)])
    for r, deal in enumerate((first, second)):
        for t in np.random.permutation(T):
            e = deal[t]; j = e * C + place[e, fill[e]]; fill[e] += 1; slot_token[j] = t; pos[r, t] = j
    g = np.random.uniform(0.2, 0.8, T)
    return {
        "xT": (n((K, T)) * s).astype(np.float32),
        "w": (n((E, K, N)) / np.sqrt(K) / s[None]).astype(np.float32),
        "b": (0.3 * n((N, E))).astype(np.float32),
        "gate": np.stack([np.tile(g, (N, 1)), np.tile(1.0 - g, (N, 1))]).astype(np.float32),
        "offs": striped(slot_token),
        "pos1": striped(pos[0]),
        "pos2": striped(pos[1]),
    }


def reference(xT, w, b, gate, offs, pos1, pos2):
    idx = unstriped(offs)
    xq = mxq(f64(xT)[:, idx], 0, "e4m3")
    y = by_expert(mxq(f64(w), 1, "e4m3"), xq)
    y = silu(y + np.repeat(f64(b), C, axis=1))
    return f64(gate[0]) * y[:, unstriped(pos1)] + f64(gate[1]) * y[:, unstriped(pos2)]

@@ -1,0 +1,134 @@
+from contextlib import ExitStack
+
+import concourse.mybir as mybir
+
+K, T, E, C, N = 512, 512, 4, 256, 128
+FLOPS = 2 * K * N * E * C
+
+F32 = mybir.dt.float32
+BF16 = mybir.dt.bfloat16
+U32 = mybir.dt.uint32
+U16 = mybir.dt.uint16
+U8 = mybir.dt.uint8
+FP8X4 = mybir.dt.float8_e4m3fn_x4
+MULT = mybir.AluOpType.mult
+ADD = mybir.AluOpType.add
+SILU = mybir.ActivationFunctionType.Silu
+COPY = mybir.ActivationFunctionType.Copy
+
+P = 128
+
+V_SPLIT = 160
+
+
+def tile_routed_moe_kernel(tc, xT, w, b, gate, offs, pos1, pos2, out):
+    nc = tc.nc
+    with ExitStack() as ctx:
+        lists = ctx.enter_context(tc.tile_pool(name="lists", bufs=1))
+        sb = ctx.enter_context(tc.tile_pool(name="sb", bufs=1))
+        ps = ctx.enter_context(tc.psum_pool(name="ps", bufs=1))
+
+        offs_sb = lists.tile([P, E * C // 16], U16, name="offs_sb")
+        pos1_sb = lists.tile([P, T // 16], U16, name="pos1_sb")
+        pos2_sb = lists.tile([P, T // 16], U16, name="pos2_sb")
+
+        nc.sync.dma_start(offs_sb[:], offs)
+        x_view = xT.rearrange("(p t) n -> t p n", t=4)
+        plane = []
+        for t in range(4):
+            r = sb.tile([P, T], F32, name="plane%d" % t)
+            nc.sync.dma_start(r[:], x_view[t])
+            plane.append(r)
+        w_raw = []
+        for e in range(E):
+            r = sb.tile([P, 4, N], F32, name="w_raw%d" % e)
+            nc.sync.dma_start(r[:], w[e].rearrange("(p j) n -> p j n", j=4))
+            w_raw.append(r)
+        b_sb = sb.tile([P, E], F32, name="b_sb")
+        nc.sync.dma_start(b_sb[:], b)
+        gate_sb = sb.tile([P, 2, T], F32, name="gate_sb")
+        nc.sync.dma_start(gate_sb[:], gate.rearrange("r n t -> n r t"))
+        nc.sync.dma_start(pos1_sb[:], pos1)
+        nc.sync.dma_start(pos2_sb[:], pos2)
+
+        warm = sb.tile([P, 2], F32, name="warm")
+        nc.gpsimd.memset(warm[:, 0:1], 0.0)
+        nc.scalar.activation(warm[:, 1:2], warm[:, 0:1], SILU)
+
+        def slots(s):
+            return offs_sb[:, s * (C // 16) : (s + 1) * (C // 16)]
+
+        grouped = []
+        for s in range(E):
+            grouped.append(sb.tile([P, C, 4], BF16, name="grouped%d" % s, align_bytes=64))
+
+        xb = sb.tile([P, 4, T], BF16, name="xb")
+        for t in range(4):
+            nc.gpsimd.tensor_scalar(
+                out=xb[:, t, :], in0=plane[t][:], scalar1=1.0, scalar2=0.0, op0=MULT, op1=ADD
+            )
+        for t in range(4):
+            nc.scalar.activation(grouped[0][:, :, t], xb[:, t, :].indirect(slots(0)), COPY)
+
+        w_grouped = sb.tile([P, E, N, 4], BF16, name="w_grouped", align_bytes=64)
+        for e in range(E):
+            nc.gpsimd.tensor_scalar(
+                out=w_grouped[:, e, :, :],
+                in0=w_raw[e][:].rearrange("p j n -> p n j"),
+                scalar1=1.0,
+                scalar2=0.0,
+                op0=MULT,
+                op1=ADD,
+            )
+
+        gx = [None]
+        for s in range(1, E):
+            gx.append(sb.tile([P, 4, C], F32, name="gx%d" % s))
+
+        def interleave(copy, s, c0, c1):
+            copy(out=grouped[s][:, c0:c1, :], in_=gx[s][:, :, c0:c1].rearrange("p t c -> p c t"))
+
+        for s in range(1, E):
+            for t in range(4):
+                nc.vector.tensor_copy(gx[s][:, t, :], plane[t][:].indirect(slots(s)))
+            if s < E - 1:
+                interleave(nc.scalar.copy, s, 0, C)
+        interleave(nc.vector.tensor_copy, E - 1, 0, V_SPLIT)
+        interleave(nc.scalar.copy, E - 1, V_SPLIT, C)
+
+        w_codes = sb.tile([P, E * N], U32, name="w_codes", align_bytes=64)
+        w_scales = sb.tile([P, E * N], U8, name="w_scales", align_bytes=64)
+        nc.vector.quantize_mx(
+            out=w_codes[:].bitcast(FP8X4),
+            scales=w_scales[:],
+            in_=w_grouped[:].rearrange("p e n j -> p (e n j)"),
+        )
+
+        y = sb.tile([P, E * C], F32, name="y")
+        for s in range(E):
+            x_codes = sb.tile([P, C], U32, name="x_codes%d" % s, align_bytes=64)
+            x_scales = sb.tile([P, C], U8, name="x_scales%d" % s, align_bytes=64)
+            nc.vector.quantize_mx(
+                out=x_codes[:].bitcast(FP8X4),
+                scales=x_scales[:],
+                in_=grouped[s][:].rearrange("p c t -> p (c t)"),
+            )
+            acc = ps.tile([P, C], F32, name="acc%d" % s)
+            nc.tensor.matmul_mx(
+                out=acc[:],
+                lhsT=w_codes[:, s * N : (s + 1) * N].bitcast(FP8X4),
+                lhsT_scale=w_scales[:, s * N : (s + 1) * N],
+                rhs=x_codes[:].bitcast(FP8X4),
+                rhs_scale=x_scales[:],
+                start=True,
+                stop=True,
+            )
+            nc.scalar.activation(y[:, s * C : (s + 1) * C], acc[:], SILU, bias=b_sb[:, s : s + 1])
+
+        o1 = sb.tile([P, T], F32, name="o1")
+        o2 = sb.tile([P, T], F32, name="o2")
+        res = sb.tile([P, T], F32, name="res")
+        nc.vector.tensor_tensor(o1[:], y[:].indirect(pos1_sb[:]), gate_sb[:, 0, :], MULT)
+        nc.vector.tensor_tensor(o2[:], y[:].indirect(pos2_sb[:]), gate_sb[:, 1, :], MULT)
+        nc.vector.tensor_tensor(res[:], o1[:], o2[:], ADD)
+        nc.sync.dma_start(out, res[:])

@@ -18,9 +18,6 @@ COPY = mybir.ActivationFunctionType.Copy
 
 P = 128
 
-V_SPLIT = 160
-
-
 def tile_routed_moe_kernel(tc, xT, w, b, gate, offs, pos1, pos2, out):
     nc = tc.nc
     with ExitStack() as ctx:
@@ -59,19 +56,37 @@ def tile_routed_moe_kernel(tc, xT, w, b, gate, offs, pos1, pos2, out):
             return offs_sb[:, s * (C // 16) : (s + 1) * (C // 16)]
 
         grouped = []
+        gx = []
+        x_codes = []
+        x_scales = []
+        acc = []
         for s in range(E):
             grouped.append(sb.tile([P, C, 4], BF16, name="grouped%d" % s, align_bytes=64))
-
+            gx.append(sb.tile([P, 4, C], F32, name="gx%d" % s))
+            x_codes.append(sb.tile([P, C], U32, name="x_codes%d" % s, align_bytes=64))
+            x_scales.append(sb.tile([P, C], U8, name="x_scales%d" % s, align_bytes=64))
+            acc.append(ps.tile([P, C], F32, name="acc%d" % s))
         xb = sb.tile([P, 4, T], BF16, name="xb")
-        for t in range(4):
+        w_grouped = sb.tile([P, E, N, 4], BF16, name="w_grouped", align_bytes=64)
+        w_codes = sb.tile([P, E * N], U32, name="w_codes", align_bytes=64)
+        w_scales = sb.tile([P, E * N], U8, name="w_scales", align_bytes=64)
+        y = sb.tile([P, E * C], F32, name="y")
+
+        def cast_plane(t):
             nc.gpsimd.tensor_scalar(
                 out=xb[:, t, :], in0=plane[t][:], scalar1=1.0, scalar2=0.0, op0=MULT, op1=ADD
             )
-        for t in range(4):
-            nc.scalar.activation(grouped[0][:, :, t], xb[:, t, :].indirect(slots(0)), COPY)
 
-        w_grouped = sb.tile([P, E, N, 4], BF16, name="w_grouped", align_bytes=64)
-        for e in range(E):
+        def gather_scalar(s, t):
+            nc.scalar.activation(grouped[s][:, :, t], xb[:, t, :].indirect(slots(s)), COPY)
+
+        def gather_vector(s, t):
+            nc.vector.tensor_copy(gx[s][:, t, :], plane[t][:].indirect(slots(s)))
+
+        def interleave(copy, s, c0, c1):
+            copy(out=grouped[s][:, c0:c1, :], in_=gx[s][:, :, c0:c1].rearrange("p t c -> p c t"))
+
+        def interleave_w(e):
             nc.gpsimd.tensor_scalar(
                 out=w_grouped[:, e, :, :],
                 in0=w_raw[e][:].rearrange("p j n -> p n j"),
@@ -81,49 +96,56 @@ def tile_routed_moe_kernel(tc, xT, w, b, gate, offs, pos1, pos2, out):
                 op1=ADD,
             )
 
-        gx = [None]
-        for s in range(1, E):
-            gx.append(sb.tile([P, 4, C], F32, name="gx%d" % s))
-
-        def interleave(copy, s, c0, c1):
-            copy(out=grouped[s][:, c0:c1, :], in_=gx[s][:, :, c0:c1].rearrange("p t c -> p c t"))
-
-        for s in range(1, E):
-            for t in range(4):
-                nc.vector.tensor_copy(gx[s][:, t, :], plane[t][:].indirect(slots(s)))
-            if s < E - 1:
-                interleave(nc.scalar.copy, s, 0, C)
-        interleave(nc.vector.tensor_copy, E - 1, 0, V_SPLIT)
-        interleave(nc.scalar.copy, E - 1, V_SPLIT, C)
-
-        w_codes = sb.tile([P, E * N], U32, name="w_codes", align_bytes=64)
-        w_scales = sb.tile([P, E * N], U8, name="w_scales", align_bytes=64)
-        nc.vector.quantize_mx(
-            out=w_codes[:].bitcast(FP8X4),
-            scales=w_scales[:],
-            in_=w_grouped[:].rearrange("p e n j -> p (e n j)"),
-        )
-
-        y = sb.tile([P, E * C], F32, name="y")
-        for s in range(E):
-            x_codes = sb.tile([P, C], U32, name="x_codes%d" % s, align_bytes=64)
-            x_scales = sb.tile([P, C], U8, name="x_scales%d" % s, align_bytes=64)
+        def quantize_w():
             nc.vector.quantize_mx(
-                out=x_codes[:].bitcast(FP8X4),
-                scales=x_scales[:],
+                out=w_codes[:].bitcast(FP8X4),
+                scales=w_scales[:],
+                in_=w_grouped[:].rearrange("p e n j -> p (e n j)"),
+            )
+
+        def quantize_x(s):
+            nc.vector.quantize_mx(
+                out=x_codes[s][:].bitcast(FP8X4),
+                scales=x_scales[s][:],
                 in_=grouped[s][:].rearrange("p c t -> p (c t)"),
             )
-            acc = ps.tile([P, C], F32, name="acc%d" % s)
+
+        def expert(s):
             nc.tensor.matmul_mx(
-                out=acc[:],
+                out=acc[s][:],
                 lhsT=w_codes[:, s * N : (s + 1) * N].bitcast(FP8X4),
                 lhsT_scale=w_scales[:, s * N : (s + 1) * N],
-                rhs=x_codes[:].bitcast(FP8X4),
-                rhs_scale=x_scales[:],
+                rhs=x_codes[s][:].bitcast(FP8X4),
+                rhs_scale=x_scales[s][:],
                 start=True,
                 stop=True,
             )
-            nc.scalar.activation(y[:, s * C : (s + 1) * C], acc[:], SILU, bias=b_sb[:, s : s + 1])
+            nc.scalar.activation(y[:, s * C : (s + 1) * C], acc[s][:], SILU, bias=b_sb[:, s : s + 1])
+
+        for t in range(4):
+            cast_plane(t)
+        for e in range(E):
+            interleave_w(e)
+        for t in range(4):
+            gather_vector(2, t)
+            gather_scalar(0, t)
+        gather_vector(3, 0)
+        interleave(nc.vector.tensor_copy, 2, 0, C)
+        quantize_x(0)
+        gather_vector(3, 1)
+        quantize_x(2)
+        gather_vector(3, 2)
+        quantize_w()
+        expert(0)
+        expert(2)
+        gather_vector(3, 3)
+        for t in range(4):
+            gather_scalar(1, t)
+        interleave(nc.vector.tensor_copy, 3, 0, C)
+        quantize_x(3)
+        expert(3)
+        quantize_x(1)
+        expert(1)
 
         o1 = sb.tile([P, T], F32, name="o1")
         o2 = sb.tile([P, T], F32, name="o2")

@@ -122,35 +122,42 @@ def tile_routed_moe_kernel(tc, xT, w, b, gate, offs, pos1, pos2, out):
             )
             nc.scalar.activation(y[:, s * C : (s + 1) * C], acc[s][:], SILU, bias=b_sb[:, s : s + 1])
 
-        for t in range(4):
+        nc.vector.tensor_copy(xb[:, 0, :], plane[0][:])
+        for t in range(1, 4):
             cast_plane(t)
         for e in range(E):
             interleave_w(e)
         for t in range(4):
             gather_vector(2, t)
             gather_scalar(0, t)
-        gather_vector(3, 0)
-        interleave(nc.vector.tensor_copy, 2, 0, C)
-        quantize_x(0)
-        gather_vector(3, 1)
-        quantize_x(2)
-        gather_vector(3, 2)
-        quantize_w()
-        expert(0)
-        expert(2)
-        gather_vector(3, 3)
         for t in range(4):
+            gather_vector(3, t)
             gather_scalar(1, t)
+        interleave(nc.vector.tensor_copy, 2, 0, C)
         interleave(nc.vector.tensor_copy, 3, 0, C)
+        quantize_w()
+        quantize_x(0)
+        expert(0)
+        quantize_x(2)
+        expert(2)
         quantize_x(3)
         expert(3)
         quantize_x(1)
         expert(1)
 
+        H = T // 2
         o1 = sb.tile([P, T], F32, name="o1")
         o2 = sb.tile([P, T], F32, name="o2")
         res = sb.tile([P, T], F32, name="res")
         nc.vector.tensor_tensor(o1[:], y[:].indirect(pos1_sb[:]), gate_sb[:, 0, :], MULT)
-        nc.vector.tensor_tensor(o2[:], y[:].indirect(pos2_sb[:]), gate_sb[:, 1, :], MULT)
-        nc.vector.tensor_tensor(res[:], o1[:], o2[:], ADD)
-        nc.sync.dma_start(out, res[:])
+        for h in range(2):
+            nc.vector.tensor_tensor(
+                o2[:, h * H : (h + 1) * H],
+                y[:].indirect(pos2_sb[:, h * (H // 16) : (h + 1) * (H // 16)]),
+                gate_sb[:, 1, h * H : (h + 1) * H],
+                MULT,
+            )
+        for h in range(2):
+            cols = slice(h * H, (h + 1) * H)
+            nc.vector.tensor_tensor(res[:, cols], o1[:, cols], o2[:, cols], ADD)
+            nc.sync.dma_start(out[:, cols], res[:, cols])

@@ -29,13 +29,14 @@ def tile_routed_moe_kernel(tc, xT, w, b, gate, offs, pos1, pos2, out):
         pos1_sb = lists.tile([P, T // 16], U16, name="pos1_sb")
         pos2_sb = lists.tile([P, T // 16], U16, name="pos2_sb")
 
-        nc.sync.dma_start(offs_sb[:], offs)
         x_view = xT.rearrange("(p t) n -> t p n", t=4)
         plane = []
         for t in range(4):
             r = sb.tile([P, T], F32, name="plane%d" % t)
             nc.sync.dma_start(r[:], x_view[t])
             plane.append(r)
+            if t == 0:
+                nc.sync.dma_start(offs_sb[:], offs)
         w_raw = []
         for e in range(E):
             r = sb.tile([P, 4, N], F32, name="w_raw%d" % e)
@@ -84,7 +85,10 @@ def tile_routed_moe_kernel(tc, xT, w, b, gate, offs, pos1, pos2, out):
             nc.vector.tensor_copy(gx[s][:, t, :], plane[t][:].indirect(slots(s)))
 
         def interleave(copy, s, c0, c1):
-            copy(out=grouped[s][:, c0:c1, :], in_=gx[s][:, :, c0:c1].rearrange("p t c -> p c t"))
+            copy(
+                out=grouped[s][:, c0:c1, :].rearrange("p (c i) t -> p c t i", i=4),
+                in_=gx[s][:, :, c0:c1].rearrange("p t (c i) -> p c t i", i=4),
+            )
 
         def interleave_w(e):
             nc.gpsimd.tensor_scalar(

@@ -17,151 +17,119 @@ SILU = mybir.ActivationFunctionType.Silu
 COPY = mybir.ActivationFunctionType.Copy
 
 P = 128
+PACK = 4
+PER_COLUMN = 16
+LINE = 4
+HALF = T // 2
+
+SCALAR_EXPERTS = (0, 1)
+VECTOR_EXPERTS = (2, 3)
+QUANTISE_ORDER = (0, 2, 3, 1)
+
 
 def tile_routed_moe_kernel(tc, xT, w, b, gate, offs, pos1, pos2, out):
     nc = tc.nc
     with ExitStack() as ctx:
         lists = ctx.enter_context(tc.tile_pool(name="lists", bufs=1))
-        sb = ctx.enter_context(tc.tile_pool(name="sb", bufs=1))
-        ps = ctx.enter_context(tc.psum_pool(name="ps", bufs=1))
+        sbuf = ctx.enter_context(tc.tile_pool(name="sbuf", bufs=1))
+        psum = ctx.enter_context(tc.psum_pool(name="psum", bufs=1))
 
-        offs_sb = lists.tile([P, E * C // 16], U16, name="offs_sb")
-        pos1_sb = lists.tile([P, T // 16], U16, name="pos1_sb")
-        pos2_sb = lists.tile([P, T // 16], U16, name="pos2_sb")
+        offs_sb = lists.tile([P, E * C // PER_COLUMN], U16, name="offs_sb")
+        pos1_sb = lists.tile([P, T // PER_COLUMN], U16, name="pos1_sb")
+        pos2_sb = lists.tile([P, T // PER_COLUMN], U16, name="pos2_sb")
 
-        x_view = xT.rearrange("(p t) n -> t p n", t=4)
+        planes_in_hbm = xT.rearrange("(p t) n -> t p n", t=PACK)
         plane = []
-        for t in range(4):
-            r = sb.tile([P, T], F32, name="plane%d" % t)
-            nc.sync.dma_start(r[:], x_view[t])
-            plane.append(r)
+        for t in range(PACK):
+            plane.append(sbuf.tile([P, T], F32, name="plane%d" % t))
+            nc.sync.dma_start(plane[t][:], planes_in_hbm[t])
             if t == 0:
                 nc.sync.dma_start(offs_sb[:], offs)
         w_raw = []
         for e in range(E):
-            r = sb.tile([P, 4, N], F32, name="w_raw%d" % e)
-            nc.sync.dma_start(r[:], w[e].rearrange("(p j) n -> p j n", j=4))
-            w_raw.append(r)
-        b_sb = sb.tile([P, E], F32, name="b_sb")
+            w_raw.append(sbuf.tile([P, PACK, N], F32, name="w_raw%d" % e))
+            nc.sync.dma_start(w_raw[e][:], w[e].rearrange("(p t) n -> p t n", t=PACK))
+        b_sb = sbuf.tile([P, E], F32, name="b_sb")
         nc.sync.dma_start(b_sb[:], b)
-        gate_sb = sb.tile([P, 2, T], F32, name="gate_sb")
+        gate_sb = sbuf.tile([P, 2, T], F32, name="gate_sb")
         nc.sync.dma_start(gate_sb[:], gate.rearrange("r n t -> n r t"))
         nc.sync.dma_start(pos1_sb[:], pos1)
         nc.sync.dma_start(pos2_sb[:], pos2)
 
-        warm = sb.tile([P, 2], F32, name="warm")
+        warm = sbuf.tile([P, 2], F32, name="warm")
         nc.gpsimd.memset(warm[:, 0:1], 0.0)
         nc.scalar.activation(warm[:, 1:2], warm[:, 0:1], SILU)
 
-        def slots(s):
-            return offs_sb[:, s * (C // 16) : (s + 1) * (C // 16)]
+        def gpsimd_round(out_bf16, in_f32):
+            nc.gpsimd.tensor_scalar(out=out_bf16, in0=in_f32, scalar1=1.0, scalar2=0.0, op0=MULT, op1=ADD)
 
-        grouped = []
-        gx = []
-        x_codes = []
-        x_scales = []
-        acc = []
-        for s in range(E):
-            grouped.append(sb.tile([P, C, 4], BF16, name="grouped%d" % s, align_bytes=64))
-            gx.append(sb.tile([P, 4, C], F32, name="gx%d" % s))
-            x_codes.append(sb.tile([P, C], U32, name="x_codes%d" % s, align_bytes=64))
-            x_scales.append(sb.tile([P, C], U8, name="x_scales%d" % s, align_bytes=64))
-            acc.append(ps.tile([P, C], F32, name="acc%d" % s))
-        xb = sb.tile([P, 4, T], BF16, name="xb")
-        w_grouped = sb.tile([P, E, N, 4], BF16, name="w_grouped", align_bytes=64)
-        w_codes = sb.tile([P, E * N], U32, name="w_codes", align_bytes=64)
-        w_scales = sb.tile([P, E * N], U8, name="w_scales", align_bytes=64)
-        y = sb.tile([P, E * C], F32, name="y")
+        planes_bf16 = sbuf.tile([P, PACK, T], BF16, name="planes_bf16")
+        nc.vector.tensor_copy(planes_bf16[:, 0, :], plane[0][:])
+        for t in range(1, PACK):
+            gpsimd_round(planes_bf16[:, t, :], plane[t][:])
 
-        def cast_plane(t):
-            nc.gpsimd.tensor_scalar(
-                out=xb[:, t, :], in0=plane[t][:], scalar1=1.0, scalar2=0.0, op0=MULT, op1=ADD
+        w_interleaved = sbuf.tile([P, E, N, PACK], BF16, name="w_interleaved", align_bytes=64)
+        for e in range(E):
+            gpsimd_round(w_interleaved[:, e, :, :], w_raw[e][:].rearrange("p t n -> p n t"))
+
+        def slots_of(e):
+            return offs_sb[:, e * C // PER_COLUMN : (e + 1) * C // PER_COLUMN]
+
+        interleaved = {}
+        gathered = {}
+        for e in range(E):
+            interleaved[e] = sbuf.tile([P, C, PACK], BF16, name="interleaved%d" % e, align_bytes=64)
+        for e in VECTOR_EXPERTS:
+            gathered[e] = sbuf.tile([P, PACK, C], F32, name="gathered%d" % e)
+
+        for on_vector, on_scalar in zip(VECTOR_EXPERTS, SCALAR_EXPERTS):
+            for t in range(PACK):
+                nc.vector.tensor_copy(gathered[on_vector][:, t, :], plane[t][:].indirect(slots_of(on_vector)))
+                nc.scalar.activation(
+                    interleaved[on_scalar][:, :, t], planes_bf16[:, t, :].indirect(slots_of(on_scalar)), COPY
+                )
+
+        for e in VECTOR_EXPERTS:
+            nc.vector.tensor_copy(
+                out=interleaved[e][:].rearrange("p (c i) t -> p c t i", i=LINE),
+                in_=gathered[e][:].rearrange("p t (c i) -> p c t i", i=LINE),
             )
 
-        def gather_scalar(s, t):
-            nc.scalar.activation(grouped[s][:, :, t], xb[:, t, :].indirect(slots(s)), COPY)
+        def quantise(name, width, in_bf16):
+            codes = sbuf.tile([P, width], U32, name="codes_%s" % name, align_bytes=64)
+            scales = sbuf.tile([P, width], U8, name="scales_%s" % name, align_bytes=64)
+            nc.vector.quantize_mx(out=codes[:].bitcast(FP8X4), scales=scales[:], in_=in_bf16)
+            return codes, scales
 
-        def gather_vector(s, t):
-            nc.vector.tensor_copy(gx[s][:, t, :], plane[t][:].indirect(slots(s)))
+        w_codes, w_scales = quantise("w", E * N, w_interleaved[:].rearrange("p e n t -> p (e n t)"))
 
-        def interleave(copy, s, c0, c1):
-            copy(
-                out=grouped[s][:, c0:c1, :].rearrange("p (c i) t -> p c t i", i=4),
-                in_=gx[s][:, :, c0:c1].rearrange("p t (c i) -> p c t i", i=4),
-            )
-
-        def interleave_w(e):
-            nc.gpsimd.tensor_scalar(
-                out=w_grouped[:, e, :, :],
-                in0=w_raw[e][:].rearrange("p j n -> p n j"),
-                scalar1=1.0,
-                scalar2=0.0,
-                op0=MULT,
-                op1=ADD,
-            )
-
-        def quantize_w():
-            nc.vector.quantize_mx(
-                out=w_codes[:].bitcast(FP8X4),
-                scales=w_scales[:],
-                in_=w_grouped[:].rearrange("p e n j -> p (e n j)"),
-            )
-
-        def quantize_x(s):
-            nc.vector.quantize_mx(
-                out=x_codes[s][:].bitcast(FP8X4),
-                scales=x_scales[s][:],
-                in_=grouped[s][:].rearrange("p c t -> p (c t)"),
-            )
-
-        def expert(s):
+        y = sbuf.tile([P, E * C], F32, name="y")
+        for e in QUANTISE_ORDER:
+            x_codes, x_scales = quantise("x%d" % e, C, interleaved[e][:].rearrange("p c t -> p (c t)"))
+            sums = psum.tile([P, C], F32, name="sums%d" % e)
             nc.tensor.matmul_mx(
-                out=acc[s][:],
-                lhsT=w_codes[:, s * N : (s + 1) * N].bitcast(FP8X4),
-                lhsT_scale=w_scales[:, s * N : (s + 1) * N],
-                rhs=x_codes[s][:].bitcast(FP8X4),
-                rhs_scale=x_scales[s][:],
+                out=sums[:],
+                lhsT=w_codes[:, e * N : (e + 1) * N].bitcast(FP8X4),
+                lhsT_scale=w_scales[:, e * N : (e + 1) * N],
+                rhs=x_codes[:].bitcast(FP8X4),
+                rhs_scale=x_scales[:],
                 start=True,
                 stop=True,
             )
-            nc.scalar.activation(y[:, s * C : (s + 1) * C], acc[s][:], SILU, bias=b_sb[:, s : s + 1])
+            nc.scalar.activation(y[:, e * C : (e + 1) * C], sums[:], SILU, bias=b_sb[:, e : e + 1])
 
-        nc.vector.tensor_copy(xb[:, 0, :], plane[0][:])
-        for t in range(1, 4):
-            cast_plane(t)
-        for e in range(E):
-            interleave_w(e)
-        for t in range(4):
-            gather_vector(2, t)
-            gather_scalar(0, t)
-        for t in range(4):
-            gather_vector(3, t)
-            gather_scalar(1, t)
-        interleave(nc.vector.tensor_copy, 2, 0, C)
-        interleave(nc.vector.tensor_copy, 3, 0, C)
-        quantize_w()
-        quantize_x(0)
-        expert(0)
-        quantize_x(2)
-        expert(2)
-        quantize_x(3)
-        expert(3)
-        quantize_x(1)
-        expert(1)
-
-        H = T // 2
-        o1 = sb.tile([P, T], F32, name="o1")
-        o2 = sb.tile([P, T], F32, name="o2")
-        res = sb.tile([P, T], F32, name="res")
-        nc.vector.tensor_tensor(o1[:], y[:].indirect(pos1_sb[:]), gate_sb[:, 0, :], MULT)
-        for h in range(2):
+        first = sbuf.tile([P, T], F32, name="first")
+        second = sbuf.tile([P, T], F32, name="second")
+        result = sbuf.tile([P, T], F32, name="result")
+        nc.vector.tensor_tensor(first[:], y[:].indirect(pos1_sb[:]), gate_sb[:, 0, :], MULT)
+        halves = [slice(h * HALF, (h + 1) * HALF) for h in range(T // HALF)]
+        for h, tokens in enumerate(halves):
             nc.vector.tensor_tensor(
-                o2[:, h * H : (h + 1) * H],
-                y[:].indirect(pos2_sb[:, h * (H // 16) : (h + 1) * (H // 16)]),
-                gate_sb[:, 1, h * H : (h + 1) * H],
+                second[:, tokens],
+                y[:].indirect(pos2_sb[:, h * HALF // PER_COLUMN : (h + 1) * HALF // PER_COLUMN]),
+                gate_sb[:, 1, tokens],
                 MULT,
             )
-        for h in range(2):
-            cols = slice(h * H, (h + 1) * H)
-            nc.vector.tensor_tensor(res[:, cols], o1[:, cols], o2[:, cols], ADD)
-            nc.sync.dma_start(out[:, cols], res[:, cols])
+        for tokens in halves:
+            nc.vector.tensor_tensor(result[:, tokens], first[:, tokens], second[:, tokens], ADD)
+            nc.sync.dma_start(out[:, tokens], result[:, tokens])

@@ -21,10 +21,11 @@ PACK = 4
 PER_COLUMN = 16
 LINE = 4
 HALF = T // 2
+PAD = 16
 
 SCALAR_EXPERTS = (0, 1)
 VECTOR_EXPERTS = (2, 3)
-QUANTISE_ORDER = (0, 2, 3, 1)
+QUANTISE_ORDER = (2, 3, 0, 1)
 
 
 def tile_routed_moe_kernel(tc, xT, w, b, gate, offs, pos1, pos2, out):
@@ -41,8 +42,9 @@ def tile_routed_moe_kernel(tc, xT, w, b, gate, offs, pos1, pos2, out):
         planes_in_hbm = xT.rearrange("(p t) n -> t p n", t=PACK)
         plane = []
         for t in range(PACK):
-            plane.append(sbuf.tile([P, T], F32, name="plane%d" % t))
-            nc.sync.dma_start(plane[t][:], planes_in_hbm[t])
+            plane.append(sbuf.tile([P, T + PAD], F32, name="plane%d" % t))
+            nc.gpsimd.memset(plane[t][:, T : T + PAD], 0.0)
+            nc.sync.dma_start(plane[t][:, 0:T], planes_in_hbm[t])
             if t == 0:
                 nc.sync.dma_start(offs_sb[:], offs)
         w_raw = []
@@ -64,11 +66,11 @@ def tile_routed_moe_kernel(tc, xT, w, b, gate, offs, pos1, pos2, out):
             nc.gpsimd.tensor_scalar(out=out_bf16, in0=in_f32, scalar1=1.0, scalar2=0.0, op0=MULT, op1=ADD)
 
         planes_bf16 = sbuf.tile([P, PACK, T], BF16, name="planes_bf16")
-        nc.vector.tensor_copy(planes_bf16[:, 0, :], plane[0][:])
+        nc.vector.tensor_copy(planes_bf16[:, 0, :], plane[0][:, 0:T])
         for t in range(1, PACK):
-            gpsimd_round(planes_bf16[:, t, :], plane[t][:])
+            gpsimd_round(planes_bf16[:, t, :], plane[t][:, 0:T])
 
-        w_interleaved = sbuf.tile([P, E, N, PACK], BF16, name="w_interleaved", align_bytes=64)
+        w_interleaved = sbuf.tile([P, E, N, PACK], BF16, name="w_interleaved", tag="handed_on", align_bytes=64)
         for e in range(E):
             gpsimd_round(w_interleaved[:, e, :, :], w_raw[e][:].rearrange("p t n -> p n t"))
 
@@ -76,43 +78,46 @@ def tile_routed_moe_kernel(tc, xT, w, b, gate, offs, pos1, pos2, out):
             return offs_sb[:, e * C // PER_COLUMN : (e + 1) * C // PER_COLUMN]
 
         interleaved = {}
-        gathered = {}
         for e in range(E):
             interleaved[e] = sbuf.tile([P, C, PACK], BF16, name="interleaved%d" % e, align_bytes=64)
-        for e in VECTOR_EXPERTS:
-            gathered[e] = sbuf.tile([P, PACK, C], F32, name="gathered%d" % e)
+        gathered = sbuf.tile([P, PACK, len(VECTOR_EXPERTS) * C], F32, name="gathered")
+        vector_slots = offs_sb[:, VECTOR_EXPERTS[0] * C // PER_COLUMN : (VECTOR_EXPERTS[-1] + 1) * C // PER_COLUMN]
 
-        for on_vector, on_scalar in zip(VECTOR_EXPERTS, SCALAR_EXPERTS):
+        for t in range(PACK):
+            nc.vector.tensor_copy(gathered[:, t, :], plane[t][:].indirect(vector_slots))
+        for e in SCALAR_EXPERTS:
             for t in range(PACK):
-                nc.vector.tensor_copy(gathered[on_vector][:, t, :], plane[t][:].indirect(slots_of(on_vector)))
-                nc.scalar.activation(
-                    interleaved[on_scalar][:, :, t], planes_bf16[:, t, :].indirect(slots_of(on_scalar)), COPY
-                )
+                nc.scalar.activation(interleaved[e][:, :, t], planes_bf16[:, t, :].indirect(slots_of(e)), COPY)
 
-        for e in VECTOR_EXPERTS:
+        for i, e in enumerate(VECTOR_EXPERTS):
             nc.vector.tensor_copy(
                 out=interleaved[e][:].rearrange("p (c i) t -> p c t i", i=LINE),
-                in_=gathered[e][:].rearrange("p t (c i) -> p c t i", i=LINE),
+                in_=gathered[:, :, i * C : (i + 1) * C].rearrange("p t (c i) -> p c t i", i=LINE),
             )
 
-        def quantise(name, width, in_bf16):
-            codes = sbuf.tile([P, width], U32, name="codes_%s" % name, align_bytes=64)
-            scales = sbuf.tile([P, width], U8, name="scales_%s" % name, align_bytes=64)
-            nc.vector.quantize_mx(out=codes[:].bitcast(FP8X4), scales=scales[:], in_=in_bf16)
-            return codes, scales
-
-        w_codes, w_scales = quantise("w", E * N, w_interleaved[:].rearrange("p e n t -> p (e n t)"))
+        w_codes = sbuf.tile([P, E * N], U32, name="w_codes", align_bytes=64)
+        w_scales = sbuf.tile([P, E * N], U8, name="w_scales", align_bytes=64)
+        nc.vector.quantize_mx(
+            out=w_codes[:].bitcast(FP8X4), scales=w_scales[:], in_=w_interleaved[:].rearrange("p e n t -> p (e n t)")
+        )
+        x_codes = sbuf.tile([P, E * C], U32, name="x_codes", tag="handed_on", align_bytes=64)
+        x_scales = sbuf.tile([P, E * C], U8, name="x_scales", align_bytes=64)
 
         y = sbuf.tile([P, E * C], F32, name="y")
         for e in QUANTISE_ORDER:
-            x_codes, x_scales = quantise("x%d" % e, C, interleaved[e][:].rearrange("p c t -> p (c t)"))
+            slots = slice(e * C, (e + 1) * C)
+            nc.vector.quantize_mx(
+                out=x_codes[:, slots].bitcast(FP8X4),
+                scales=x_scales[:, slots],
+                in_=interleaved[e][:].rearrange("p c t -> p (c t)"),
+            )
             sums = psum.tile([P, C], F32, name="sums%d" % e)
             nc.tensor.matmul_mx(
                 out=sums[:],
                 lhsT=w_codes[:, e * N : (e + 1) * N].bitcast(FP8X4),
                 lhsT_scale=w_scales[:, e * N : (e + 1) * N],
-                rhs=x_codes[:].bitcast(FP8X4),
-                rhs_scale=x_scales[:],
+                rhs=x_codes[:, slots].bitcast(FP8X4),
+                rhs_scale=x_scales[:, slots],
                 start=True,
                 stop=True,
             )

@@ -21,11 +21,12 @@ PACK = 4
 PER_COLUMN = 16
 LINE = 4
 HALF = T // 2
-PAD = 16
 
-SCALAR_EXPERTS = (0, 1)
-VECTOR_EXPERTS = (2, 3)
-QUANTISE_ORDER = (2, 3, 0, 1)
+SCALAR_SLOTS = 512
+VECTOR_SLOTS = E * C - SCALAR_SLOTS
+PAD = max(VECTOR_SLOTS - T, 0) + 16
+SCALAR_PIECES = [(e * C, min((e + 1) * C, SCALAR_SLOTS)) for e in range(E) if e * C < SCALAR_SLOTS]
+QUANTISE_ORDER = [e for e in range(E) if e * C >= SCALAR_SLOTS] + [e for e in range(E) if e * C < SCALAR_SLOTS]
 
 
 def tile_routed_moe_kernel(tc, xT, w, b, gate, offs, pos1, pos2, out):
@@ -67,33 +68,29 @@ def tile_routed_moe_kernel(tc, xT, w, b, gate, offs, pos1, pos2, out):
 
         planes_bf16 = sbuf.tile([P, PACK, T], BF16, name="planes_bf16")
         nc.vector.tensor_copy(planes_bf16[:, 0, :], plane[0][:, 0:T])
-        for t in range(1, PACK):
+        for t in range(1, PACK - 1):
             gpsimd_round(planes_bf16[:, t, :], plane[t][:, 0:T])
+        nc.scalar.activation(planes_bf16[:, PACK - 1, :], plane[PACK - 1][:, 0:T], COPY)
 
         w_interleaved = sbuf.tile([P, E, N, PACK], BF16, name="w_interleaved", tag="handed_on", align_bytes=64)
         for e in range(E):
             gpsimd_round(w_interleaved[:, e, :, :], w_raw[e][:].rearrange("p t n -> p n t"))
 
-        def slots_of(e):
-            return offs_sb[:, e * C // PER_COLUMN : (e + 1) * C // PER_COLUMN]
-
-        interleaved = {}
-        for e in range(E):
-            interleaved[e] = sbuf.tile([P, C, PACK], BF16, name="interleaved%d" % e, align_bytes=64)
-        gathered = sbuf.tile([P, PACK, len(VECTOR_EXPERTS) * C], F32, name="gathered")
-        vector_slots = offs_sb[:, VECTOR_EXPERTS[0] * C // PER_COLUMN : (VECTOR_EXPERTS[-1] + 1) * C // PER_COLUMN]
-
+        interleaved = sbuf.tile([P, E * C, PACK], BF16, name="interleaved", align_bytes=64)
+        gathered = sbuf.tile([P, PACK, VECTOR_SLOTS], F32, name="gathered")
         for t in range(PACK):
-            nc.vector.tensor_copy(gathered[:, t, :], plane[t][:].indirect(vector_slots))
-        for e in SCALAR_EXPERTS:
+            nc.vector.tensor_copy(gathered[:, t, :], plane[t][:].indirect(offs_sb[:, SCALAR_SLOTS // PER_COLUMN :]))
+        for lo, hi in SCALAR_PIECES:
             for t in range(PACK):
-                nc.scalar.activation(interleaved[e][:, :, t], planes_bf16[:, t, :].indirect(slots_of(e)), COPY)
-
-        for i, e in enumerate(VECTOR_EXPERTS):
-            nc.vector.tensor_copy(
-                out=interleaved[e][:].rearrange("p (c i) t -> p c t i", i=LINE),
-                in_=gathered[:, :, i * C : (i + 1) * C].rearrange("p t (c i) -> p c t i", i=LINE),
-            )
+                nc.scalar.activation(
+                    interleaved[:, lo:hi, t],
+                    planes_bf16[:, t, :].indirect(offs_sb[:, lo // PER_COLUMN : hi // PER_COLUMN]),
+                    COPY,
+                )
+        nc.vector.tensor_copy(
+            out=interleaved[:, SCALAR_SLOTS:, :].rearrange("p (c i) t -> p c t i", i=LINE),
+            in_=gathered[:].rearrange("p t (c i) -> p c t i", i=LINE),
+        )
 
         w_codes = sbuf.tile([P, E * N], U32, name="w_codes", align_bytes=64)
         w_scales = sbuf.tile([P, E * N], U8, name="w_scales", align_bytes=64)
@@ -109,7 +106,7 @@ def tile_routed_moe_kernel(tc, xT, w, b, gate, offs, pos1, pos2, out):
             nc.vector.quantize_mx(
                 out=x_codes[:, slots].bitcast(FP8X4),
                 scales=x_scales[:, slots],
-                in_=interleaved[e][:].rearrange("p c t -> p (c t)"),
+                in_=interleaved[:, slots, :].rearrange("p c t -> p (c t)"),
             )
             sums = psum.tile([P, C], F32, name="sums%d" % e)
             nc.tensor.matmul_mx(
@@ -121,7 +118,7 @@ def tile_routed_moe_kernel(tc, xT, w, b, gate, offs, pos1, pos2, out):
                 start=True,
                 stop=True,
             )
-            nc.scalar.activation(y[:, e * C : (e + 1) * C], sums[:], SILU, bias=b_sb[:, e : e + 1])
+            nc.scalar.activation(y[:, slots], sums[:], SILU, bias=b_sb[:, e : e + 1])
 
         first = sbuf.tile([P, T], F32, name="first")
         second = sbuf.tile([P, T], F32, name="second")

@@ -74,7 +74,10 @@ def tile_routed_moe_kernel(tc, xT, w, b, gate, offs, pos1, pos2, out):
 
         w_interleaved = sbuf.tile([P, E, N, PACK], BF16, name="w_interleaved", tag="handed_on", align_bytes=64)
         for e in range(E):
-            gpsimd_round(w_interleaved[:, e, :, :], w_raw[e][:].rearrange("p t n -> p n t"))
+            gpsimd_round(
+                w_interleaved[:, e, :, :].rearrange("p (n i) t -> p n t i", i=LINE),
+                w_raw[e][:].rearrange("p t (n i) -> p n t i", i=LINE),
+            )
 
         interleaved = sbuf.tile([P, E * C, PACK], BF16, name="interleaved", align_bytes=64)
         gathered = sbuf.tile([P, PACK, VECTOR_SLOTS], F32, name="gathered")

@@ -25,7 +25,7 @@ HALF = T // 2
 SCALAR_SLOTS = 512
 VECTOR_SLOTS = E * C - SCALAR_SLOTS
 PAD = max(VECTOR_SLOTS - T, 0) + 16
-SCALAR_PIECES = [(e * C, min((e + 1) * C, SCALAR_SLOTS)) for e in range(E) if e * C < SCALAR_SLOTS]
+SCALAR_PIECES = [(0, C), (C, C + C // 2), (C + C // 2, 2 * C)]
 QUANTISE_ORDER = [e for e in range(E) if e * C >= SCALAR_SLOTS] + [e for e in range(E) if e * C < SCALAR_SLOTS]
 
 
@@ -104,14 +104,15 @@ def tile_routed_moe_kernel(tc, xT, w, b, gate, offs, pos1, pos2, out):
         x_scales = sbuf.tile([P, E * C], U8, name="x_scales", align_bytes=64)
 
         y = sbuf.tile([P, E * C], F32, name="y")
-        for e in QUANTISE_ORDER:
-            slots = slice(e * C, (e + 1) * C)
+        pieces = [(e, 0, C) for e in QUANTISE_ORDER[:-1]] + [(QUANTISE_ORDER[-1], h * C // 2, C // 2) for h in range(2)]
+        for e, start, width in pieces:
+            slots = slice(e * C + start, e * C + start + width)
             nc.vector.quantize_mx(
                 out=x_codes[:, slots].bitcast(FP8X4),
                 scales=x_scales[:, slots],
                 in_=interleaved[:, slots, :].rearrange("p c t -> p (c t)"),
             )
-            sums = psum.tile([P, C], F32, name="sums%d" % e)
+            sums = psum.tile([P, width], F32, name="sums%d_%d" % (e, start))
             nc.tensor.matmul_mx(
                 out=sums[:],
                 lhsT=w_codes[:, e * N : (e + 1) * N].bitcast(FP8X4),

@@ -45,9 +45,12 @@ def tile_routed_moe_kernel(tc, xT, w, b, gate, offs, pos1, pos2, out):
         for t in range(PACK):
             plane.append(sbuf.tile([P, T + PAD], F32, name="plane%d" % t))
             nc.gpsimd.memset(plane[t][:, T : T + PAD], 0.0)
-            nc.sync.dma_start(plane[t][:, 0:T], planes_in_hbm[t])
             if t == 0:
+                nc.sync.dma_start(plane[t][:, 0:HALF], planes_in_hbm[t][:, 0:HALF])
+                nc.sync.dma_start(plane[t][:, HALF:T], planes_in_hbm[t][:, HALF:T])
                 nc.sync.dma_start(offs_sb[:], offs)
+            else:
+                nc.sync.dma_start(plane[t][:, 0:T], planes_in_hbm[t])
         w_raw = []
         for e in range(E):
             w_raw.append(sbuf.tile([P, PACK, N], F32, name="w_raw%d" % e))
@@ -67,7 +70,8 @@ def tile_routed_moe_kernel(tc, xT, w, b, gate, offs, pos1, pos2, out):
             nc.gpsimd.tensor_scalar(out=out_bf16, in0=in_f32, scalar1=1.0, scalar2=0.0, op0=MULT, op1=ADD)
 
         planes_bf16 = sbuf.tile([P, PACK, T], BF16, name="planes_bf16")
-        nc.vector.tensor_copy(planes_bf16[:, 0, :], plane[0][:, 0:T])
+        nc.vector.tensor_copy(planes_bf16[:, 0, 0:HALF], plane[0][:, 0:HALF])
+        nc.vector.tensor_copy(planes_bf16[:, 0, HALF:T], plane[0][:, HALF:T])
         for t in range(1, PACK - 1):
             gpsimd_round(planes_bf16[:, t, :], plane[t][:, 0:T])
         nc.scalar.activation(planes_bf16[:, PACK - 1, :], plane[PACK - 1][:, 0:T], COPY)

@@ -49,12 +49,14 @@ def tile_routed_moe_kernel(tc, xT, w, b, gate, offs, pos1, pos2, out):
                 nc.sync.dma_start(plane[t][:, 0:HALF], planes_in_hbm[t][:, 0:HALF])
                 nc.sync.dma_start(plane[t][:, HALF:T], planes_in_hbm[t][:, HALF:T])
                 nc.sync.dma_start(offs_sb[:], offs)
-            else:
+            elif t < PACK - 1:
                 nc.sync.dma_start(plane[t][:, 0:T], planes_in_hbm[t])
         w_raw = []
         for e in range(E):
             w_raw.append(sbuf.tile([P, PACK, N], F32, name="w_raw%d" % e))
             nc.sync.dma_start(w_raw[e][:], w[e].rearrange("(p t) n -> p t n", t=PACK))
+            if e == 0:
+                nc.sync.dma_start(plane[PACK - 1][:, 0:T], planes_in_hbm[PACK - 1])
         b_sb = sbuf.tile([P, E], F32, name="b_sb")
         nc.sync.dma_start(b_sb[:], b)
         gate_sb = sbuf.tile([P, 2, T], F32, name="gate_sb")

from contextlib import ExitStack

import concourse.mybir as mybir

K, T, E, C, N = 512, 512, 4, 256, 128
FLOPS = 2 * K * N * E * C

F32 = mybir.dt.float32
BF16 = mybir.dt.bfloat16
U32 = mybir.dt.uint32
U16 = mybir.dt.uint16
U8 = mybir.dt.uint8
FP8X4 = mybir.dt.float8_e4m3fn_x4
MULT = mybir.AluOpType.mult
ADD = mybir.AluOpType.add
SILU = mybir.ActivationFunctionType.Silu
COPY = mybir.ActivationFunctionType.Copy

P = 128
PACK = 4
PER_COLUMN = 16
LINE = 4
HALF = T // 2

SCALAR_SLOTS = 512
VECTOR_SLOTS = E * C - SCALAR_SLOTS
PAD = max(VECTOR_SLOTS - T, 0) + 16
SCALAR_PIECES = [(0, C), (C, C + C // 2), (C + C // 2, 2 * C)]
QUANTISE_ORDER = [e for e in range(E) if e * C >= SCALAR_SLOTS] + [e for e in range(E) if e * C < SCALAR_SLOTS]


def tile_routed_moe_kernel(tc, xT, w, b, gate, offs, pos1, pos2, out):
    nc = tc.nc
    with ExitStack() as ctx:
        lists = ctx.enter_context(tc.tile_pool(name="lists", bufs=1))
        sbuf = ctx.enter_context(tc.tile_pool(name="sbuf", bufs=1))
        psum = ctx.enter_context(tc.psum_pool(name="psum", bufs=1))

        offs_sb = lists.tile([P, E * C // PER_COLUMN], U16, name="offs_sb")
        pos1_sb = lists.tile([P, T // PER_COLUMN], U16, name="pos1_sb")
        pos2_sb = lists.tile([P, T // PER_COLUMN], U16, name="pos2_sb")

        planes_in_hbm = xT.rearrange("(p t) n -> t p n", t=PACK)
        plane = []
        for t in range(PACK):
            plane.append(sbuf.tile([P, T + PAD], F32, name="plane%d" % t))
            nc.gpsimd.memset(plane[t][:, T : T + PAD], 0.0)
            if t == 0:
                nc.sync.dma_start(plane[t][:, 0:HALF], planes_in_hbm[t][:, 0:HALF])
                nc.sync.dma_start(plane[t][:, HALF:T], planes_in_hbm[t][:, HALF:T])
                nc.sync.dma_start(offs_sb[:], offs)
            elif t < PACK - 1:
                nc.sync.dma_start(plane[t][:, 0:T], planes_in_hbm[t])
        w_raw = []
        for e in range(E):
            w_raw.append(sbuf.tile([P, PACK, N], F32, name="w_raw%d" % e))
            nc.sync.dma_start(w_raw[e][:], w[e].rearrange("(p t) n -> p t n", t=PACK))
            if e == 0:
                nc.sync.dma_start(plane[PACK - 1][:, 0:T], planes_in_hbm[PACK - 1])
        b_sb = sbuf.tile([P, E], F32, name="b_sb")
        nc.sync.dma_start(b_sb[:], b)
        gate_sb = sbuf.tile([P, 2, T], F32, name="gate_sb")
        nc.sync.dma_start(gate_sb[:], gate.rearrange("r n t -> n r t"))
        nc.sync.dma_start(pos1_sb[:], pos1)
        nc.sync.dma_start(pos2_sb[:], pos2)

        warm = sbuf.tile([P, 2], F32, name="warm")
        nc.gpsimd.memset(warm[:, 0:1], 0.0)
        nc.scalar.activation(warm[:, 1:2], warm[:, 0:1], SILU)

        def gpsimd_round(out_bf16, in_f32):
            nc.gpsimd.tensor_scalar(out=out_bf16, in0=in_f32, scalar1=1.0, scalar2=0.0, op0=MULT, op1=ADD)

        planes_bf16 = sbuf.tile([P, PACK, T], BF16, name="planes_bf16")
        nc.vector.tensor_copy(planes_bf16[:, 0, 0:HALF], plane[0][:, 0:HALF])
        nc.vector.tensor_copy(planes_bf16[:, 0, HALF:T], plane[0][:, HALF:T])
        for t in range(1, PACK - 1):
            gpsimd_round(planes_bf16[:, t, :], plane[t][:, 0:T])
        nc.scalar.activation(planes_bf16[:, PACK - 1, :], plane[PACK - 1][:, 0:T], COPY)

        w_interleaved = sbuf.tile([P, E, N, PACK], BF16, name="w_interleaved", tag="handed_on", align_bytes=64)
        for e in range(E):
            gpsimd_round(
                w_interleaved[:, e, :, :].rearrange("p (n i) t -> p n t i", i=LINE),
                w_raw[e][:].rearrange("p t (n i) -> p n t i", i=LINE),
            )

        interleaved = sbuf.tile([P, E * C, PACK], BF16, name="interleaved", align_bytes=64)
        gathered = sbuf.tile([P, PACK, VECTOR_SLOTS], F32, name="gathered")
        for t in range(PACK):
            nc.vector.tensor_copy(gathered[:, t, :], plane[t][:].indirect(offs_sb[:, SCALAR_SLOTS // PER_COLUMN :]))
        for lo, hi in SCALAR_PIECES:
            for t in range(PACK):
                nc.scalar.activation(
                    interleaved[:, lo:hi, t],
                    planes_bf16[:, t, :].indirect(offs_sb[:, lo // PER_COLUMN : hi // PER_COLUMN]),
                    COPY,
                )
        nc.vector.tensor_copy(
            out=interleaved[:, SCALAR_SLOTS:, :].rearrange("p (c i) t -> p c t i", i=LINE),
            in_=gathered[:].rearrange("p t (c i) -> p c t i", i=LINE),
        )

        w_codes = sbuf.tile([P, E * N], U32, name="w_codes", align_bytes=64)
        w_scales = sbuf.tile([P, E * N], U8, name="w_scales", align_bytes=64)
        nc.vector.quantize_mx(
            out=w_codes[:].bitcast(FP8X4), scales=w_scales[:], in_=w_interleaved[:].rearrange("p e n t -> p (e n t)")
        )
        x_codes = sbuf.tile([P, E * C], U32, name="x_codes", tag="handed_on", align_bytes=64)
        x_scales = sbuf.tile([P, E * C], U8, name="x_scales", align_bytes=64)

        y = sbuf.tile([P, E * C], F32, name="y")
        pieces = [(e, 0, C) for e in QUANTISE_ORDER[:-1]] + [(QUANTISE_ORDER[-1], h * C // 2, C // 2) for h in range(2)]
        for e, start, width in pieces:
            slots = slice(e * C + start, e * C + start + width)
            nc.vector.quantize_mx(
                out=x_codes[:, slots].bitcast(FP8X4),
                scales=x_scales[:, slots],
                in_=interleaved[:, slots, :].rearrange("p c t -> p (c t)"),
            )
            sums = psum.tile([P, width], F32, name="sums%d_%d" % (e, start))
            nc.tensor.matmul_mx(
                out=sums[:],
                lhsT=w_codes[:, e * N : (e + 1) * N].bitcast(FP8X4),
                lhsT_scale=w_scales[:, e * N : (e + 1) * N],
                rhs=x_codes[:, slots].bitcast(FP8X4),
                rhs_scale=x_scales[:, slots],
                start=True,
                stop=True,
            )
            nc.scalar.activation(y[:, slots], sums[:], SILU, bias=b_sb[:, e : e + 1])

        first = sbuf.tile([P, T], F32, name="first")
        second = sbuf.tile([P, T], F32, name="second")
        result = sbuf.tile([P, T], F32, name="result")
        nc.vector.tensor_tensor(first[:], y[:].indirect(pos1_sb[:]), gate_sb[:, 0, :], MULT)
        halves = [slice(h * HALF, (h + 1) * HALF) for h in range(T // HALF)]
        for h, tokens in enumerate(halves):
            nc.vector.tensor_tensor(
                second[:, tokens],
                y[:].indirect(pos2_sb[:, h * HALF // PER_COLUMN : (h + 1) * HALF // PER_COLUMN]),
                gate_sb[:, 1, tokens],
                MULT,
            )
        for tokens in halves:
            nc.vector.tensor_tensor(result[:, tokens], first[:, tokens], second[:, tokens], ADD)
            nc.sync.dma_start(out[:, tokens], result[:, tokens])
